import numpy as np
import ml_dtypes


def mxq(x, axis, fmt="e4m3"):
    dtype, down = {"e4m3": (ml_dtypes.float8_e4m3fn, 7), "e5m2": (ml_dtypes.float8_e5m2, 14)}[fmt]
    v = np.moveaxis(np.asarray(x, np.float32).astype(ml_dtypes.bfloat16).astype(np.float64), axis, -1)
    blocks = v.reshape(v.shape[:-1] + (-1, 32))
    amax = np.abs(blocks).max(-1, keepdims=True)
    byte = np.maximum(np.where(amax > 0, np.frexp(amax)[1] - 1 + 127, 0) - down, 1)
    scale = np.exp2(byte - 127.0)
    codes = (blocks / scale).astype(np.float32).astype(dtype).astype(np.float64)
    return np.moveaxis((codes * scale).reshape(v.shape), -1, axis)


WIDE = False


def mx_kscale(k):
    if not WIDE:
        return np.ones(k)
    levels = np.array([10, -10, 5, -5, 0])
    if k % 512:
        return np.exp2(np.random.permutation(np.resize(levels, k // 32))).repeat(32)
    a = np.empty((k // 512, 16))
    for p in range(k // 512):
        a[p, :8] = np.random.permutation(np.resize(levels, 8))
        for g in range(8):
            far = levels[np.abs(levels - a[p, g]) >= 10]
            a[p, g + 8] = far[np.random.randint(len(far))]
    return np.exp2(a.ravel()).repeat(32)


def f64(x):
    return np.asarray(x).astype(np.float64)


E2M1 = np.array([0.0, 0.5, 1.0, 1.5, 2.0, 3.0, 4.0, 6.0, -0.0, -0.5, -1.0, -1.5, -2.0, -3.0, -4.0, -6.0])


def pack_weight(w, fmt):
    k, n = w.shape
    w = f64(np.asarray(w, np.float32).astype(ml_dtypes.bfloat16)).reshape(k // 32, 32, n)
    amax = np.abs(w).max(1)
    if fmt == "e4m3":
        byte = np.frexp(amax)[1] - 1 + 127 - 7
    else:
        mant, ex = np.frexp(amax / 6.0)
        byte = np.where(mant > 0.5, ex, ex - 1) + 127
    byte = np.clip(np.where(amax > 0, byte, 1), 1, 254)
    scaled = (w * np.exp2(127.0 - byte)[:, None, :]).reshape(k, n).astype(np.float32)
    by_word = np.ascontiguousarray(scaled.reshape(k // 512, 128, 4, n).transpose(0, 1, 3, 2))
    if fmt == "e4m3":
        words = by_word.astype(ml_dtypes.float8_e4m3fn).view(np.uint8)
    else:
        c = by_word.astype(ml_dtypes.float4_e2m1fn).view(np.uint8) & 0xF
        words = (c[..., 0::2] | (c[..., 1::2] << 4)).reshape(k // 512, 128, 2 * n)
    return np.ascontiguousarray(words), np.ascontiguousarray(byte.astype(np.uint8).reshape(k // 512, 16, n))


def unpack_weight(words, scales, fmt):
    g, _, n = scales.shape
    words = np.ascontiguousarray(words).reshape(g, 128, n, -1)
    if fmt == "e4m3":
        vals = words.view(ml_dtypes.float8_e4m3fn).astype(np.float64)
    else:
        nib = np.empty((g, 128, n, 4), np.uint8)
        nib[..., 0::2] = words & 0xF
        nib[..., 1::2] = words >> 4
        vals = E2M1[nib]
    vals = vals * np.repeat(np.exp2(scales.astype(np.float64) - 127.0), 8, axis=1)[..., None]
    return vals.transpose(0, 1, 3, 2).reshape(g * 512, n)


def planes(y):
    n, m = y.shape
    v = y.astype(np.float32).astype(ml_dtypes.bfloat16).astype(np.float64).reshape(n // 32, 32, m)
    top = np.abs(v).max(1)
    byte = np.clip(np.where(top > 0, np.frexp(top)[1] - 1 + 127 - 7, 1), 1, 254)
    codes = (v * np.exp2(127.0 - byte)[:, None, :]).reshape(n, m).astype(np.float32).astype(ml_dtypes.float8_e4m3fn).view(np.uint8)
    words = codes.reshape(n // 512, 128, 4, m).transpose(0, 1, 3, 2)
    return np.ascontiguousarray(words), np.ascontiguousarray(byte.astype(np.uint8).reshape(n // 512, 16, m))


K, M, T = 1024, 1024, 512


def setup_inputs():
    n = np.random.standard_normal
    s = mx_kscale(K)[:, None]
    u = mx_kscale(T)[:, None]
    q = n((K, T)) * s
    p_vc = pack_weight(0.1 * n((T, M)) / u, "e2m1")
    return {
        "qc": (q).astype(np.float32),
        "kc": (n((K, T)) / np.sqrt(K) / s).astype(np.float32),
        "qd": (q * 0.995 ** (np.arange(T) + 1.0)).astype(np.float32),
        "st": (n((K, M)) / np.sqrt(K) / s).astype(np.float32),
        "vc_words": p_vc[0],
        "vc_scales": p_vc[1],
        "dm": (np.tril(0.995 ** (np.arange(T)[:, None] - np.arange(T)[None])).T * u).astype(np.float32),
    }


def reference(qc, kc, qd, st, vc_words, vc_scales, dm):
    qc_ = mxq(f64(qc), 0, "e4m3")
    kc_ = mxq(f64(kc), 0, "e4m3")
    qd_ = mxq(f64(qd), 0, "e4m3")
    st_ = mxq(f64(st), 0, "e4m3")
    vc_ = unpack_weight(vc_words, vc_scales, "e2m1")
    h_ = mxq((kc_.T @ qc_) * f64(dm), 0, "e4m3")
    y = h_.T @ vc_ + qd_.T @ st_
    out_0 = y
    return (out_0,) + planes(out_0)

@@ -1,0 +1,202 @@
+from contextlib import ExitStack
+
+import concourse.mybir as mybir
+
+K, M, T = 1024, 1024, 512
+FLOPS = 2 * (K * T * T + T * T * M + K * T * M)
+
+F32 = mybir.dt.float32
+BF16 = mybir.dt.bfloat16
+I32 = mybir.dt.int32
+U32 = mybir.dt.uint32
+U8 = mybir.dt.uint8
+FP8X4 = mybir.dt.float8_e4m3fn_x4
+FP4X4 = mybir.dt.float4_e2m1fn_x4
+
+P = 128
+PACK = 4
+K_PASS = P * PACK
+PASSES = K // K_PASS
+HALF = T // 2
+BANK_N = 128
+CHUNK = 256
+CHUNKS = M // CHUNK
+BANKS = M // BANK_N
+
+
+def tile_mix_linattn_tm_pl_none_kernel(tc, qc, kc, qd, st, vc_words, vc_scales, dm, out_0, out_1, out_2):
+    nc = tc.nc
+
+    with ExitStack() as ctx:
+        sb = ctx.enter_context(tc.tile_pool(name="sb", bufs=1))
+        psum = ctx.enter_context(tc.psum_pool(name="psum", bufs=1))
+        ctx.enter_context(tc.manual_schedule())
+
+        def load_rows(name, rows):
+            raw = sb.tile([P, PACK, rows.shape[1]], F32, name=name)
+            nc.sync.dma_start(out=raw[:], in_=rows.rearrange("(p j) w -> p j w", j=PACK))
+            return raw
+
+        def pass_rows(a):
+            return slice(a * K_PASS, (a + 1) * K_PASS)
+
+        def operand(name, width):
+            codes = sb.tile([P, width], U32, name=name + "_codes", align_bytes=64)
+            scales = sb.tile([P, width], U8, name=name + "_scales", align_bytes=64)
+            return codes, scales
+
+        def copy_on(engine, out, in_):
+            if engine == "scalar":
+                nc.scalar.copy(out=out, in_=in_)
+            else:
+                nc.vector.tensor_copy(out=out, in_=in_)
+
+        def interleave(engine, name, src):
+            width = src.shape[2]
+            grouped = sb.tile([P, width, PACK], BF16, name=name, align_bytes=64)
+            copy_on(
+                engine,
+                grouped[:].rearrange("p (c i) j -> p c j i", i=4),
+                src.rearrange("p j (c i) -> p c j i", i=4),
+            )
+            return grouped[:].rearrange("p w j -> p (w j)")
+
+        def deal(engine, name, src, half):
+            grouped = sb.tile([P, 2, P, PACK], BF16, name=name, align_bytes=64)
+            copy_on(
+                engine,
+                grouped[:].rearrange("p r m j -> p m j r"),
+                src.rearrange("p j (m r) -> p m j r", r=4)[:, :, :, 2 * half : 2 * half + 2],
+            )
+            return grouped[:].rearrange("p r m j -> p (r m j)")
+
+        def quantize(dst, cols, grouped):
+            codes, scales = dst
+            nc.vector.quantize_mx(out=codes[:, cols].bitcast(FP8X4), scales=scales[:, cols], in_=grouped)
+
+        def prepare(name, src, dealt):
+            dst = operand(name, T)
+            lo, hi = slice(0, HALF), slice(HALF, T)
+            if dealt:
+                g_lo = deal("scalar", name + "_lo", src, 0)
+                g_hi = deal("vector", name + "_hi", src, 1)
+            else:
+                g_lo = interleave("scalar", name + "_lo", src[:, :, lo])
+                g_hi = interleave("vector", name + "_hi", src[:, :, hi])
+            quantize(dst, hi, g_hi)
+            quantize(dst, lo, g_lo)
+            return dst
+
+        def mx(out, lhs, lhs_cols, rhs, rhs_scale, start, stop):
+            codes, scales = lhs
+            nc.tensor.matmul_mx(
+                out=out,
+                lhsT=codes[:, lhs_cols].bitcast(FP8X4),
+                lhsT_scale=scales[:, lhs_cols],
+                rhs=rhs,
+                rhs_scale=rhs_scale,
+                start=start,
+                stop=stop,
+            )
+
+        def block(r):
+            return slice(r * P, (r + 1) * P)
+
+        v_scales = sb.tile([P, M], U8, name="v_scales", align_bytes=64)
+        nc.vector.memset(v_scales[:].bitcast(I32), 0)
+        kc_raw, qc_raw = [], []
+        for a in range(PASSES):
+            kc_raw.append(load_rows("kc_raw%d" % a, kc[pass_rows(a), :]))
+            if a == 0:
+                for q in range(4):
+                    nc.scalar.dma_start(
+                        out=v_scales[32 * q : 32 * q + 4, :].bitcast(I32),
+                        in_=vc_scales[0, 4 * q : 4 * q + 4, :].bitcast(I32),
+                    )
+            qc_raw.append(load_rows("qc_raw%d" % a, qc[pass_rows(a), :]))
+        dm_raw = load_rows("dm_raw", dm)
+        v_words = sb.tile([P, 2 * M], U8, name="v_words", align_bytes=64)
+        nc.sync.dma_start(out=v_words[:].bitcast(I32), in_=vc_words[0].bitcast(I32))
+        qd_raw = [load_rows("qd_raw%d" % a, qd[pass_rows(a), :]) for a in range(PASSES)]
+        st_raw = [
+            [load_rows("st_raw%d_%d" % (c, a), st[pass_rows(a), c * CHUNK : (c + 1) * CHUNK]) for a in range(PASSES)]
+            for c in range(CHUNKS)
+        ]
+
+        h_sum = []
+        for i in range(PACK):
+            bank = psum.tile([P, T], F32, name="h_sum%d" % i, tag="bank%d" % (BANKS - PACK + i))
+            h_sum.append(bank)
+        for a in range(PASSES):
+            k_op = prepare("kc%d" % a, kc_raw[a][:], True)
+            q_codes, q_scales = prepare("qc%d" % a, qc_raw[a][:], False)
+            for i in range(PACK):
+                mx(h_sum[i][:], k_op, block(i), q_codes[:].bitcast(FP8X4), q_scales[:], a == 0, a == PASSES - 1)
+        h_rows = sb.tile([P, PACK, T], BF16, name="h_rows")
+        for i in range(PACK):
+            nc.vector.tensor_tensor(out=h_rows[:, i, :], in0=h_sum[i][:], in1=dm_raw[:, i, :], op=mybir.AluOpType.mult)
+        h_op = prepare("h", h_rows[:], True)
+
+        acc = []
+        for b in range(BANKS):
+            bank = psum.tile([P, PACK, BANK_N], F32, name="acc%d" % b, tag="bank%d" % b)
+            acc.append(bank)
+            cols = slice(b * BANK_N, (b + 1) * BANK_N)
+            words = v_words[:, 2 * b * BANK_N : 2 * (b + 1) * BANK_N].bitcast(FP4X4)
+            for r in range(PACK):
+                mx(bank[:, r, :], h_op, block(r), words, v_scales[:, cols], r == 0, False)
+
+        qd_op = [prepare("qd%d" % a, qd_raw[a][:], True) for a in range(PASSES)]
+
+        out_rows = out_0.rearrange("(p r) n -> p r n", r=PACK)
+        out_words = out_1[0].rearrange("p n t -> p (n t)")
+        o_op = operand("o", M)
+        o_codes, o_scales = o_op
+        o_grouped = {}
+
+        def chunk_cols(c):
+            return slice(c * CHUNK, (c + 1) * CHUNK)
+
+        def multiply(c):
+            grouped = [
+                interleave(engine, "st_g%d_%d" % (c, a), st_raw[c][a][:])
+                for a, engine in enumerate(("scalar", "vector"))
+            ]
+            for a in range(PASSES):
+                s_op = operand("st%d_%d" % (c, a), CHUNK)
+                quantize(s_op, slice(0, CHUNK), grouped[a])
+                s_codes, s_scales = s_op
+                for u in range(CHUNK // BANK_N):
+                    bank = acc[c * (CHUNK // BANK_N) + u]
+                    cols = slice(u * BANK_N, (u + 1) * BANK_N)
+                    for r in range(PACK):
+                        last = a == PASSES - 1 and r == PACK - 1
+                        mx(bank[:, r, :], qd_op[a], block(r), s_codes[:, cols].bitcast(FP8X4), s_scales[:, cols], False, last)
+
+        def drain(c):
+            result = sb.tile([P, PACK, CHUNK], F32, name="result%d" % c)
+            for u in range(CHUNK // BANK_N):
+                nc.scalar.copy(out=result[:, :, u * BANK_N : (u + 1) * BANK_N], in_=acc[c * (CHUNK // BANK_N) + u][:])
+            nc.sync.dma_start(out=out_rows[:, :, chunk_cols(c)], in_=result[:])
+            o_grouped[c] = interleave("vector", "o_g%d" % c, result[:])
+
+        def planes(c):
+            quantize(o_op, chunk_cols(c), o_grouped[c])
+            if c % 2 == 1:
+                n0, n1 = (c - 1) * CHUNK, (c + 1) * CHUNK
+                nc.sync.dma_start(out=out_words[:, 4 * n0 : 4 * n1].bitcast(I32), in_=o_codes[:, n0:n1].bitcast(I32))
+
+        for c in range(CHUNKS + 2):
+            if c < CHUNKS:
+                multiply(c)
+            if 0 <= c - 2:
+                planes(c - 2)
+            if 0 <= c - 1 < CHUNKS:
+                drain(c - 1)
+
+        for q in range(4):
+            queue = nc.scalar if q % 2 == 0 else nc.sync
+            queue.dma_start(
+                out=out_2[0, 4 * q : 4 * q + 4, :].bitcast(I32),
+                in_=o_scales[32 * q : 32 * q + 4, :].bitcast(I32),
+            )

@@ -74,18 +74,23 @@ def tile_mix_linattn_tm_pl_none_kernel(tc, qc, kc, qd, st, vc_words, vc_scales, 
             codes, scales = dst
             nc.vector.quantize_mx(out=codes[:, cols].bitcast(FP8X4), scales=scales[:, cols], in_=grouped)
 
-        def prepare(name, src, dealt):
-            dst = operand(name, T)
-            lo, hi = slice(0, HALF), slice(HALF, T)
+        def round_halves(name, src, dealt):
             if dealt:
                 g_lo = deal("scalar", name + "_lo", src, 0)
                 g_hi = deal("vector", name + "_hi", src, 1)
             else:
-                g_lo = interleave("scalar", name + "_lo", src[:, :, lo])
-                g_hi = interleave("vector", name + "_hi", src[:, :, hi])
-            quantize(dst, hi, g_hi)
-            quantize(dst, lo, g_lo)
+                g_lo = interleave("scalar", name + "_lo", src[:, :, :HALF])
+                g_hi = interleave("vector", name + "_hi", src[:, :, HALF:])
+            return g_lo, g_hi
+
+        def quantize_halves(name, halves):
+            dst = operand(name, T)
+            quantize(dst, slice(HALF, T), halves[1])
+            quantize(dst, slice(0, HALF), halves[0])
             return dst
+
+        def prepare(name, src, dealt):
+            return quantize_halves(name, round_halves(name, src, dealt))
 
         def mx(out, lhs, lhs_cols, rhs, rhs_scale, start, stop):
             codes, scales = lhs
@@ -104,20 +109,19 @@ def tile_mix_linattn_tm_pl_none_kernel(tc, qc, kc, qd, st, vc_words, vc_scales, 
 
         v_scales = sb.tile([P, M], U8, name="v_scales", align_bytes=64)
         nc.vector.memset(v_scales[:].bitcast(I32), 0)
+        for q in range(4):
+            nc.gpsimd.dma_start(
+                out=v_scales[32 * q : 32 * q + 4, :].bitcast(I32),
+                in_=vc_scales[0, 4 * q : 4 * q + 4, :].bitcast(I32),
+            )
         kc_raw, qc_raw = [], []
         for a in range(PASSES):
             kc_raw.append(load_rows("kc_raw%d" % a, kc[pass_rows(a), :]))
-            if a == 0:
-                for q in range(4):
-                    nc.scalar.dma_start(
-                        out=v_scales[32 * q : 32 * q + 4, :].bitcast(I32),
-                        in_=vc_scales[0, 4 * q : 4 * q + 4, :].bitcast(I32),
-                    )
             qc_raw.append(load_rows("qc_raw%d" % a, qc[pass_rows(a), :]))
         dm_raw = load_rows("dm_raw", dm)
+        qd_raw = [load_rows("qd_raw%d" % a, qd[pass_rows(a), :]) for a in range(PASSES)]
         v_words = sb.tile([P, 2 * M], U8, name="v_words", align_bytes=64)
         nc.sync.dma_start(out=v_words[:].bitcast(I32), in_=vc_words[0].bitcast(I32))
-        qd_raw = [load_rows("qd_raw%d" % a, qd[pass_rows(a), :]) for a in range(PASSES)]
         st_raw = [
             [load_rows("st_raw%d_%d" % (c, a), st[pass_rows(a), c * CHUNK : (c + 1) * CHUNK]) for a in range(PASSES)]
             for c in range(CHUNKS)
@@ -135,68 +139,122 @@ def tile_mix_linattn_tm_pl_none_kernel(tc, qc, kc, qd, st, vc_words, vc_scales, 
         h_rows = sb.tile([P, PACK, T], BF16, name="h_rows")
         for i in range(PACK):
             nc.vector.tensor_tensor(out=h_rows[:, i, :], in0=h_sum[i][:], in1=dm_raw[:, i, :], op=mybir.AluOpType.mult)
-        h_op = prepare("h", h_rows[:], True)
+        qd0_halves = round_halves("qd0", qd_raw[0][:], True)
+        h_halves = round_halves("h", h_rows[:], True)
+        qd_op = [quantize_halves("qd0", qd0_halves)]
+        h_op = quantize_halves("h", h_halves)
 
         acc = []
-        for b in range(BANKS):
-            bank = psum.tile([P, PACK, BANK_N], F32, name="acc%d" % b, tag="bank%d" % b)
-            acc.append(bank)
-            cols = slice(b * BANK_N, (b + 1) * BANK_N)
-            words = v_words[:, 2 * b * BANK_N : 2 * (b + 1) * BANK_N].bitcast(FP4X4)
-            for r in range(PACK):
-                mx(bank[:, r, :], h_op, block(r), words, v_scales[:, cols], r == 0, False)
 
-        qd_op = [prepare("qd%d" % a, qd_raw[a][:], True) for a in range(PASSES)]
+        def open_banks(c):
+            for b in chunk_banks(c):
+                bank = psum.tile([P, PACK, BANK_N], F32, name="acc%d" % b, tag="bank%d" % b)
+                acc.append(bank)
+                words = v_words[:, 2 * b * BANK_N : 2 * (b + 1) * BANK_N].bitcast(FP4X4)
+                for r in range(PACK):
+                    mx(bank[:, r, :], h_op, block(r), words, v_scales[:, block(b)], r == 0, False)
+
+        def chunk_banks(c):
+            return range(2 * c, 2 * c + 2)
+
+        def chunk_cols(c):
+            return slice(c * CHUNK, (c + 1) * CHUNK)
+
+        open_banks(0)
+        open_banks(1)
+        qd_op.append(prepare("qd1", qd_raw[1][:], True))
 
         out_rows = out_0.rearrange("(p r) n -> p r n", r=PACK)
         out_words = out_1[0].rearrange("p n t -> p (n t)")
         o_op = operand("o", M)
         o_codes, o_scales = o_op
-        o_grouped = {}
-
-        def chunk_cols(c):
-            return slice(c * CHUNK, (c + 1) * CHUNK)
-
-        def multiply(c):
-            grouped = [
-                interleave(engine, "st_g%d_%d" % (c, a), st_raw[c][a][:])
-                for a, engine in enumerate(("scalar", "vector"))
-            ]
-            for a in range(PASSES):
-                s_op = operand("st%d_%d" % (c, a), CHUNK)
-                quantize(s_op, slice(0, CHUNK), grouped[a])
-                s_codes, s_scales = s_op
-                for u in range(CHUNK // BANK_N):
-                    bank = acc[c * (CHUNK // BANK_N) + u]
-                    cols = slice(u * BANK_N, (u + 1) * BANK_N)
-                    for r in range(PACK):
-                        last = a == PASSES - 1 and r == PACK - 1
-                        mx(bank[:, r, :], qd_op[a], block(r), s_codes[:, cols].bitcast(FP8X4), s_scales[:, cols], False, last)
-
-        def drain(c):
+        results, o_grouped = [], []
+        for c in range(CHUNKS):
             result = sb.tile([P, PACK, CHUNK], F32, name="result%d" % c)
-            for u in range(CHUNK // BANK_N):
-                nc.scalar.copy(out=result[:, :, u * BANK_N : (u + 1) * BANK_N], in_=acc[c * (CHUNK // BANK_N) + u][:])
-            nc.sync.dma_start(out=out_rows[:, :, chunk_cols(c)], in_=result[:])
-            o_grouped[c] = interleave("vector", "o_g%d" % c, result[:])
+            results.append(result)
+            grouped = sb.tile([P, CHUNK, PACK], BF16, name="o_g%d" % c, align_bytes=64)
+            o_grouped.append(grouped)
 
-        def planes(c):
-            quantize(o_op, chunk_cols(c), o_grouped[c])
-            if c % 2 == 1:
-                n0, n1 = (c - 1) * CHUNK, (c + 1) * CHUNK
-                nc.sync.dma_start(out=out_words[:, 4 * n0 : 4 * n1].bitcast(I32), in_=o_codes[:, n0:n1].bitcast(I32))
+        def round_state(engine, c, a, cols):
+            return interleave(engine, "st_g%d_%d_%d" % (c, a, cols.start), st_raw[c][a][:, :, cols])
 
-        for c in range(CHUNKS + 2):
-            if c < CHUNKS:
-                multiply(c)
-            if 0 <= c - 2:
-                planes(c - 2)
-            if 0 <= c - 1 < CHUNKS:
-                drain(c - 1)
+        def multiply_state(c, a, cols, grouped):
+            width = cols.stop - cols.start
+            s_op = operand("st%d_%d_%d" % (c, a, cols.start), width)
+            quantize(s_op, slice(0, width), grouped)
+            s_codes, s_scales = s_op
+            for u in range(width // BANK_N):
+                bank = acc[2 * c + cols.start // BANK_N + u]
+                for r in range(PACK):
+                    last = a == PASSES - 1 and r == PACK - 1
+                    mx(bank[:, r, :], qd_op[a], block(r), s_codes[:, block(u)].bitcast(FP8X4), s_scales[:, block(u)], False, last)
 
-        for q in range(4):
-            queue = nc.scalar if q % 2 == 0 else nc.sync
-            queue.dma_start(
-                out=out_2[0, 4 * q : 4 * q + 4, :].bitcast(I32),
-                in_=o_scales[32 * q : 32 * q + 4, :].bitcast(I32),
+        def copy_out(c, u):
+            nc.scalar.copy(out=results[c][:, :, block(u)], in_=acc[2 * c + u][:])
+
+        def store_result(c):
+            nc.sync.dma_start(out=out_rows[:, :, chunk_cols(c)], in_=results[c][:])
+
+        def round_from_psum(c):
+            for u in range(2):
+                nc.scalar.copy(out=o_grouped[c][:, block(u), :], in_=acc[2 * c + u][:].rearrange("p r n -> p n r"))
+
+        def round_from_sbuf(c, cols):
+            nc.vector.tensor_copy(
+                out=o_grouped[c][:, cols, :].rearrange("p (c i) j -> p c j i", i=4),
+                in_=results[c][:, :, cols].rearrange("p j (c i) -> p c j i", i=4),
             )
+
+        def quantize_result(c):
+            quantize(o_op, chunk_cols(c), o_grouped[c][:].rearrange("p n r -> p (n r)"))
+
+        def store_words(c0, c1):
+            n0, n1 = c0 * CHUNK, c1 * CHUNK
+            nc.sync.dma_start(out=out_words[:, 4 * n0 : 4 * n1].bitcast(I32), in_=o_codes[:, n0:n1].bitcast(I32))
+
+        whole = slice(0, CHUNK)
+        for c in range(2):
+            g0 = round_state("scalar", c, 0, whole)
+            g1 = round_state("vector", c, 1, whole)
+            multiply_state(c, 0, whole, g0)
+            multiply_state(c, 1, whole, g1)
+            open_banks(c + 2)
+
+        def drain_early(c):
+            copy_out(c, 0)
+            copy_out(c, 1)
+            store_result(c)
+            round_from_psum(c)
+
+        drain_early(0)
+        g0 = round_state("vector", 2, 0, whole)
+        g1 = round_state("vector", 2, 1, whole)
+        multiply_state(2, 0, whole, g0)
+        multiply_state(2, 1, whole, g1)
+        drain_early(1)
+
+        g0 = round_state("vector", 3, 0, whole)
+        quantize_result(0)
+        multiply_state(3, 0, whole, g0)
+        g1 = [round_state("vector", 3, 1, block(u)) for u in range(2)]
+        for u in range(2):
+            multiply_state(3, 1, block(u), g1[u])
+        copy_out(2, 0)
+        copy_out(2, 1)
+        quantize_result(1)
+        store_result(2)
+        store_words(0, 2)
+        round_from_sbuf(2, whole)
+        copy_out(3, 0)
+        quantize_result(2)
+        round_from_sbuf(3, block(0))
+        copy_out(3, 1)
+        store_result(3)
+        round_from_sbuf(3, block(1))
+        quantize_result(3)
+        store_words(2, 4)
+
+        scale_rows = out_2[0].rearrange("(q r) n -> r q n", r=4)
+        for r in range(4):
+            queue = nc.scalar if r % 2 == 0 else nc.sync
+            queue.dma_start(out=scale_rows[r].bitcast(I32), in_=o_scales[r:P:32, :].bitcast(I32))

from contextlib import ExitStack

import concourse.mybir as mybir

K, M, T = 1024, 1024, 512
FLOPS = 2 * (K * T * T + T * T * M + K * T * M)

F32 = mybir.dt.float32
BF16 = mybir.dt.bfloat16
I32 = mybir.dt.int32
U32 = mybir.dt.uint32
U8 = mybir.dt.uint8
FP8X4 = mybir.dt.float8_e4m3fn_x4
FP4X4 = mybir.dt.float4_e2m1fn_x4

P = 128
PACK = 4
K_PASS = P * PACK
PASSES = K // K_PASS
HALF = T // 2
BANK_N = 128
CHUNK = 256
CHUNKS = M // CHUNK
BANKS = M // BANK_N


def tile_mix_linattn_tm_pl_none_kernel(tc, qc, kc, qd, st, vc_words, vc_scales, dm, out_0, out_1, out_2):
    nc = tc.nc

    with ExitStack() as ctx:
        sb = ctx.enter_context(tc.tile_pool(name="sb", bufs=1))
        psum = ctx.enter_context(tc.psum_pool(name="psum", bufs=1))
        ctx.enter_context(tc.manual_schedule())

        def load_rows(name, rows):
            raw = sb.tile([P, PACK, rows.shape[1]], F32, name=name)
            nc.sync.dma_start(out=raw[:], in_=rows.rearrange("(p j) w -> p j w", j=PACK))
            return raw

        def pass_rows(a):
            return slice(a * K_PASS, (a + 1) * K_PASS)

        def operand(name, width):
            codes = sb.tile([P, width], U32, name=name + "_codes", align_bytes=64)
            scales = sb.tile([P, width], U8, name=name + "_scales", align_bytes=64)
            return codes, scales

        def copy_on(engine, out, in_):
            if engine == "scalar":
                nc.scalar.copy(out=out, in_=in_)
            else:
                nc.vector.tensor_copy(out=out, in_=in_)

        def interleave(engine, name, src):
            width = src.shape[2]
            grouped = sb.tile([P, width, PACK], BF16, name=name, align_bytes=64)
            copy_on(
                engine,
                grouped[:].rearrange("p (c i) j -> p c j i", i=4),
                src.rearrange("p j (c i) -> p c j i", i=4),
            )
            return grouped[:].rearrange("p w j -> p (w j)")

        def deal(engine, name, src, half):
            grouped = sb.tile([P, 2, P, PACK], BF16, name=name, align_bytes=64)
            copy_on(
                engine,
                grouped[:].rearrange("p r m j -> p m j r"),
                src.rearrange("p j (m r) -> p m j r", r=4)[:, :, :, 2 * half : 2 * half + 2],
            )
            return grouped[:].rearrange("p r m j -> p (r m j)")

        def quantize(dst, cols, grouped):
            codes, scales = dst
            nc.vector.quantize_mx(out=codes[:, cols].bitcast(FP8X4), scales=scales[:, cols], in_=grouped)

        def round_halves(name, src, dealt):
            if dealt:
                g_lo = deal("scalar", name + "_lo", src, 0)
                g_hi = deal("vector", name + "_hi", src, 1)
            else:
                g_lo = interleave("scalar", name + "_lo", src[:, :, :HALF])
                g_hi = interleave("vector", name + "_hi", src[:, :, HALF:])
            return g_lo, g_hi

        def quantize_halves(name, halves):
            dst = operand(name, T)
            quantize(dst, slice(HALF, T), halves[1])
            quantize(dst, slice(0, HALF), halves[0])
            return dst

        def prepare(name, src, dealt):
            return quantize_halves(name, round_halves(name, src, dealt))

        def mx(out, lhs, lhs_cols, rhs, rhs_scale, start, stop):
            codes, scales = lhs
            nc.tensor.matmul_mx(
                out=out,
                lhsT=codes[:, lhs_cols].bitcast(FP8X4),
                lhsT_scale=scales[:, lhs_cols],
                rhs=rhs,
                rhs_scale=rhs_scale,
                start=start,
                stop=stop,
            )

        def block(r):
            return slice(r * P, (r + 1) * P)

        v_scales = sb.tile([P, M], U8, name="v_scales", align_bytes=64)
        nc.vector.memset(v_scales[:].bitcast(I32), 0)
        for q in range(4):
            nc.gpsimd.dma_start(
                out=v_scales[32 * q : 32 * q + 4, :].bitcast(I32),
                in_=vc_scales[0, 4 * q : 4 * q + 4, :].bitcast(I32),
            )
        kc_raw, qc_raw = [], []
        for a in range(PASSES):
            kc_raw.append(load_rows("kc_raw%d" % a, kc[pass_rows(a), :]))
            qc_raw.append(load_rows("qc_raw%d" % a, qc[pass_rows(a), :]))
        dm_raw = load_rows("dm_raw", dm)
        qd_raw = [load_rows("qd_raw%d" % a, qd[pass_rows(a), :]) for a in range(PASSES)]
        v_words = sb.tile([P, 2 * M], U8, name="v_words", align_bytes=64)
        nc.sync.dma_start(out=v_words[:].bitcast(I32), in_=vc_words[0].bitcast(I32))
        st_raw = [
            [load_rows("st_raw%d_%d" % (c, a), st[pass_rows(a), c * CHUNK : (c + 1) * CHUNK]) for a in range(PASSES)]
            for c in range(CHUNKS)
        ]

        h_sum = []
        for i in range(PACK):
            bank = psum.tile([P, T], F32, name="h_sum%d" % i, tag="bank%d" % (BANKS - PACK + i))
            h_sum.append(bank)
        for a in range(PASSES):
            k_op = prepare("kc%d" % a, kc_raw[a][:], True)
            q_codes, q_scales = prepare("qc%d" % a, qc_raw[a][:], False)
            for i in range(PACK):
                mx(h_sum[i][:], k_op, block(i), q_codes[:].bitcast(FP8X4), q_scales[:], a == 0, a == PASSES - 1)
        h_rows = sb.tile([P, PACK, T], BF16, name="h_rows")
        for i in range(PACK):
            nc.vector.tensor_tensor(out=h_rows[:, i, :], in0=h_sum[i][:], in1=dm_raw[:, i, :], op=mybir.AluOpType.mult)
        qd0_halves = round_halves("qd0", qd_raw[0][:], True)
        h_halves = round_halves("h", h_rows[:], True)
        qd_op = [quantize_halves("qd0", qd0_halves)]
        h_op = quantize_halves("h", h_halves)

        acc = []

        def open_banks(c):
            for b in chunk_banks(c):
                bank = psum.tile([P, PACK, BANK_N], F32, name="acc%d" % b, tag="bank%d" % b)
                acc.append(bank)
                words = v_words[:, 2 * b * BANK_N : 2 * (b + 1) * BANK_N].bitcast(FP4X4)
                for r in range(PACK):
                    mx(bank[:, r, :], h_op, block(r), words, v_scales[:, block(b)], r == 0, False)

        def chunk_banks(c):
            return range(2 * c, 2 * c + 2)

        def chunk_cols(c):
            return slice(c * CHUNK, (c + 1) * CHUNK)

        open_banks(0)
        open_banks(1)
        qd_op.append(prepare("qd1", qd_raw[1][:], True))

        out_rows = out_0.rearrange("(p r) n -> p r n", r=PACK)
        out_words = out_1[0].rearrange("p n t -> p (n t)")
        o_op = operand("o", M)
        o_codes, o_scales = o_op
        results, o_grouped = [], []
        for c in range(CHUNKS):
            result = sb.tile([P, PACK, CHUNK], F32, name="result%d" % c)
            results.append(result)
            grouped = sb.tile([P, CHUNK, PACK], BF16, name="o_g%d" % c, align_bytes=64)
            o_grouped.append(grouped)

        def round_state(engine, c, a, cols):
            return interleave(engine, "st_g%d_%d_%d" % (c, a, cols.start), st_raw[c][a][:, :, cols])

        def multiply_state(c, a, cols, grouped):
            width = cols.stop - cols.start
            s_op = operand("st%d_%d_%d" % (c, a, cols.start), width)
            quantize(s_op, slice(0, width), grouped)
            s_codes, s_scales = s_op
            for u in range(width // BANK_N):
                bank = acc[2 * c + cols.start // BANK_N + u]
                for r in range(PACK):
                    last = a == PASSES - 1 and r == PACK - 1
                    mx(bank[:, r, :], qd_op[a], block(r), s_codes[:, block(u)].bitcast(FP8X4), s_scales[:, block(u)], False, last)

        def copy_out(c, u):
            nc.scalar.copy(out=results[c][:, :, block(u)], in_=acc[2 * c + u][:])

        def store_result(c):
            nc.sync.dma_start(out=out_rows[:, :, chunk_cols(c)], in_=results[c][:])

        def round_from_psum(c):
            for u in range(2):
                nc.scalar.copy(out=o_grouped[c][:, block(u), :], in_=acc[2 * c + u][:].rearrange("p r n -> p n r"))

        def round_from_sbuf(c, cols):
            nc.vector.tensor_copy(
                out=o_grouped[c][:, cols, :].rearrange("p (c i) j -> p c j i", i=4),
                in_=results[c][:, :, cols].rearrange("p j (c i) -> p c j i", i=4),
            )

        def quantize_result(c):
            quantize(o_op, chunk_cols(c), o_grouped[c][:].rearrange("p n r -> p (n r)"))

        def store_words(c0, c1):
            n0, n1 = c0 * CHUNK, c1 * CHUNK
            nc.sync.dma_start(out=out_words[:, 4 * n0 : 4 * n1].bitcast(I32), in_=o_codes[:, n0:n1].bitcast(I32))

        whole = slice(0, CHUNK)
        for c in range(2):
            g0 = round_state("scalar", c, 0, whole)
            g1 = round_state("vector", c, 1, whole)
            multiply_state(c, 0, whole, g0)
            multiply_state(c, 1, whole, g1)
            open_banks(c + 2)

        def drain_early(c):
            copy_out(c, 0)
            copy_out(c, 1)
            store_result(c)
            round_from_psum(c)

        drain_early(0)
        g0 = round_state("vector", 2, 0, whole)
        g1 = round_state("vector", 2, 1, whole)
        multiply_state(2, 0, whole, g0)
        multiply_state(2, 1, whole, g1)
        drain_early(1)

        g0 = round_state("vector", 3, 0, whole)
        quantize_result(0)
        multiply_state(3, 0, whole, g0)
        g1 = [round_state("vector", 3, 1, block(u)) for u in range(2)]
        for u in range(2):
            multiply_state(3, 1, block(u), g1[u])
        copy_out(2, 0)
        copy_out(2, 1)
        quantize_result(1)
        store_result(2)
        store_words(0, 2)
        round_from_sbuf(2, whole)
        copy_out(3, 0)
        quantize_result(2)
        round_from_sbuf(3, block(0))
        copy_out(3, 1)
        store_result(3)
        round_from_sbuf(3, block(1))
        quantize_result(3)
        store_words(2, 4)

        scale_rows = out_2[0].rearrange("(q r) n -> r q n", r=4)
        for r in range(4):
            queue = nc.scalar if r % 2 == 0 else nc.sync
            queue.dma_start(out=scale_rows[r].bitcast(I32), in_=o_scales[r:P:32, :].bitcast(I32))
